import numpy as np
CORES = [3,11,19,27,35,43,51,59,67,75,83,91]
N = 12
T = 128
ROUTE = [[[9],[2],[6],[11],[7],[6],[5],[0],[7],[0],[1],[0],[4],[8],[6],[7],[10],[7],[4],[2],[3],[11],[7],[9],[7],[1],[10],[5],[0],[5],[11],[8],[7],[4],[8],[7],[5],[11],[10],[2],[0],[8],[10],[0],[7],[8],[3],[8],[1],[10],[8],[6],[4],[6],[11],[7],[4],[2],[0],[9],[6],[2],[4],[10],[6],[2],[4],[10],[6],[0],[4],[0],[8],[10],[9],[4],[0],[9],[6],[7],[2],[2],[5],[3],[4],[5],[10],[3],[8],[3],[10],[4],[7],[2],[0],[5],[6],[3],[3],[6],[5],[11],[3],[0],[10],[2],[6],[6],[1],[11],[0],[4],[0],[7],[3],[5],[2],[6],[10],[0],[10],[9],[4],[4],[10],[3],[5],[6]],[[4],[0],[2],[8],[1],[9],[11],[1],[11],[4],[7],[9],[4],[9],[1],[5],[6],[7],[6],[4],[8],[7],[7],[10],[7],[0],[1],[4],[6],[6],[6],[0],[11],[9],[6],[0],[11],[3],[1],[6],[10],[1],[0],[1],[10],[3],[8],[10],[5],[11],[7],[5],[7],[8],[2],[2],[6],[8],[3],[3],[6],[4],[7],[11],[3],[0],[1],[10],[0],[9],[5],[0],[8],[2],[2],[0],[1],[11],[11],[2],[4],[0],[6],[9],[8],[9],[6],[1],[10],[5],[2],[2],[7],[8],[2],[1],[9],[5],[2],[1],[10],[2],[8],[11],[8],[11],[9],[8],[3],[3],[2],[7],[1],[1],[9],[4],[9],[3],[4],[2],[6],[1],[6],[2],[4],[4],[1],[7]],[[0],[6],[9],[9],[5],[5],[6],[3],[8],[11],[7],[9],[3],[10],[8],[4],[6],[4],[10],[4],[11],[1],[0],[9],[8],[2],[10],[4],[0],[2],[4],[0],[8],[2],[5],[7],[6],[5],[1],[3],[1],[4],[7],[5],[2],[10],[2],[1],[10],[5],[0],[9],[4],[0],[8],[0],[1],[1],[2],[4],[5],[5],[9],[11],[2],[10],[3],[9],[11],[11],[5],[9],[9],[8],[6],[11],[1],[6],[5],[11],[0],[6],[1],[9],[7],[9],[5],[11],[11],[8],[9],[10],[3],[11],[10],[3],[5],[2],[8],[11],[2],[4],[0],[9],[3],[8],[3],[0],[6],[9],[1],[9],[4],[4],[9],[3],[4],[11],[10],[1],[10],[11],[10],[4],[2],[11],[0],[4]],[[0],[0],[2],[7],[2],[4],[5],[11],[2],[4],[3],[2],[3],[10],[1],[4],[1],[6],[3],[7],[9],[9],[1],[7],[1],[7],[10],[11],[3],[4],[4],[11],[7],[2],[7],[9],[1],[7],[10],[5],[2],[2],[1],[5],[6],[9],[5],[1],[6],[3],[8],[8],[9],[8],[8],[1],[1],[9],[1],[7],[0],[2],[3],[10],[11],[11],[2],[4],[3],[8],[3],[5],[10],[3],[1],[11],[10],[11],[11],[10],[7],[10],[9],[5],[1],[4],[4],[3],[5],[3],[9],[3],[2],[10],[4],[4],[4],[2],[7],[3],[5],[11],[6],[1],[6],[2],[6],[3],[6],[5],[2],[3],[2],[5],[5],[3],[5],[11],[1],[11],[8],[5],[3],[10],[6],[9],[8],[5]],[[0],[6],[6],[10],[9],[3],[8],[6],[10],[11],[1],[6],[5],[7],[5],[5],[4],[6],[2],[11],[2],[3],[7],[2],[11],[9],[0],[9],[8],[3],[1],[2],[0],[1],[6],[2],[2],[8],[7],[5],[0],[8],[0],[6],[2],[2],[11],[8],[7],[1],[5],[2],[5],[6],[11],[7],[7],[4],[3],[11],[5],[9],[6],[10],[5],[7],[3],[2],[4],[5],[8],[7],[3],[4],[9],[5],[11],[3],[8],[8],[7],[7],[3],[5],[10],[0],[9],[11],[5],[1],[6],[6],[3],[11],[10],[5],[10],[9],[3],[11],[5],[4],[2],[7],[2],[0],[7],[1],[5],[10],[8],[5],[0],[7],[2],[9],[3],[1],[5],[1],[8],[6],[4],[4],[10],[3],[7],[7]],[[11],[8],[4],[4],[2],[8],[10],[8],[4],[9],[1],[5],[7],[3],[2],[9],[2],[6],[6],[9],[9],[10],[8],[7],[2],[11],[6],[6],[0],[2],[5],[0],[4],[5],[11],[11],[1],[5],[6],[5],[5],[8],[10],[5],[1],[9],[8],[3],[10],[2],[11],[3],[7],[5],[7],[1],[7],[10],[7],[3],[11],[10],[5],[1],[3],[5],[10],[3],[8],[11],[0],[9],[8],[5],[11],[0],[2],[4],[10],[11],[4],[2],[4],[11],[11],[0],[2],[4],[9],[8],[5],[7],[8],[1],[0],[5],[5],[1],[10],[8],[3],[5],[9],[2],[10],[4],[0],[3],[9],[10],[9],[4],[9],[7],[7],[9],[3],[9],[2],[7],[2],[8],[6],[9],[7],[6],[8],[4]],[[2],[1],[10],[8],[6],[9],[9],[3],[2],[10],[1],[2],[11],[8],[4],[1],[0],[6],[5],[1],[10],[9],[5],[4],[11],[3],[5],[10],[8],[1],[7],[11],[8],[8],[10],[10],[9],[1],[6],[3],[4],[2],[2],[9],[8],[8],[5],[8],[9],[5],[11],[1],[10],[10],[0],[5],[4],[0],[8],[0],[7],[7],[7],[6],[7],[11],[5],[1],[1],[6],[4],[0],[9],[6],[8],[4],[0],[0],[8],[8],[7],[1],[9],[1],[10],[10],[0],[7],[0],[4],[8],[6],[10],[2],[3],[1],[5],[2],[2],[5],[10],[4],[0],[0],[5],[7],[6],[6],[0],[8],[1],[9],[4],[5],[2],[3],[3],[4],[1],[6],[2],[4],[9],[5],[6],[6],[1],[4]],[[0],[0],[9],[11],[7],[7],[9],[2],[9],[11],[5],[1],[0],[5],[7],[6],[8],[7],[5],[11],[1],[10],[10],[0],[8],[7],[7],[7],[9],[6],[1],[8],[6],[3],[11],[4],[2],[6],[1],[6],[11],[9],[2],[8],[9],[10],[1],[9],[4],[0],[11],[8],[4],[2],[7],[3],[3],[8],[3],[9],[11],[4],[1],[11],[2],[4],[8],[0],[8],[6],[3],[6],[0],[1],[2],[2],[6],[4],[5],[4],[10],[6],[11],[3],[9],[8],[11],[5],[2],[9],[8],[1],[8],[5],[3],[1],[10],[2],[2],[5],[7],[3],[8],[10],[6],[5],[9],[4],[6],[2],[6],[4],[1],[5],[10],[4],[10],[4],[4],[6],[6],[10],[6],[10],[10],[11],[2],[0]],[[10],[5],[8],[8],[3],[7],[11],[10],[8],[11],[5],[6],[10],[8],[3],[10],[6],[5],[7],[8],[0],[9],[7],[11],[9],[3],[0],[7],[0],[3],[1],[0],[5],[1],[11],[3],[6],[0],[10],[4],[3],[6],[6],[9],[9],[1],[11],[8],[3],[3],[8],[8],[7],[9],[7],[4],[4],[10],[1],[6],[0],[11],[9],[5],[3],[1],[6],[2],[2],[10],[9],[9],[0],[5],[6],[0],[4],[0],[1],[2],[2],[3],[6],[0],[3],[10],[0],[2],[3],[8],[8],[0],[2],[11],[11],[0],[6],[11],[10],[5],[7],[8],[11],[9],[9],[9],[1],[6],[0],[6],[1],[6],[4],[8],[2],[7],[3],[8],[2],[5],[2],[11],[3],[3],[9],[7],[6],[4]],[[7],[0],[3],[0],[4],[10],[1],[11],[11],[4],[8],[11],[1],[0],[9],[7],[4],[6],[11],[4],[11],[6],[8],[6],[8],[1],[7],[11],[0],[2],[10],[10],[6],[1],[6],[8],[5],[11],[7],[9],[6],[7],[5],[5],[6],[6],[4],[1],[6],[11],[5],[1],[0],[10],[9],[7],[4],[0],[7],[10],[0],[6],[4],[0],[7],[9],[7],[11],[7],[5],[0],[3],[11],[8],[2],[11],[6],[10],[5],[1],[3],[3],[11],[0],[8],[2],[3],[6],[9],[11],[3],[11],[3],[7],[4],[0],[1],[5],[8],[2],[11],[2],[9],[6],[5],[3],[0],[10],[11],[2],[4],[6],[5],[2],[6],[4],[5],[5],[11],[8],[10],[7],[7],[3],[11],[3],[2],[11]],[[8],[2],[1],[7],[0],[11],[8],[1],[1],[6],[7],[6],[8],[9],[5],[1],[10],[7],[0],[4],[3],[8],[11],[1],[11],[4],[11],[11],[9],[6],[7],[6],[4],[1],[6],[6],[2],[5],[7],[9],[0],[2],[5],[2],[8],[10],[9],[1],[4],[0],[10],[8],[7],[4],[0],[0],[0],[5],[10],[8],[4],[4],[9],[2],[7],[2],[8],[2],[11],[9],[6],[6],[8],[1],[11],[10],[3],[11],[3],[5],[3],[4],[8],[3],[3],[7],[0],[9],[6],[6],[3],[10],[2],[9],[5],[1],[0],[0],[2],[9],[5],[5],[8],[10],[3],[8],[5],[1],[0],[11],[10],[3],[1],[4],[4],[6],[7],[8],[6],[11],[9],[10],[4],[2],[11],[7],[8],[2]],[[9],[10],[1],[1],[9],[1],[5],[3],[4],[3],[7],[7],[6],[8],[3],[8],[11],[9],[8],[3],[3],[3],[5],[1],[2],[1],[11],[5],[6],[3],[4],[9],[11],[8],[3],[2],[8],[6],[6],[11],[10],[1],[3],[0],[8],[10],[6],[5],[10],[11],[3],[4],[7],[9],[9],[0],[3],[4],[8],[2],[5],[11],[3],[3],[5],[1],[2],[5],[7],[9],[5],[8],[11],[9],[9],[2],[6],[9],[2],[2],[2],[8],[9],[5],[7],[6],[6],[1],[10],[9],[0],[2],[2],[7],[10],[6],[3],[3],[7],[1],[6],[7],[4],[8],[0],[7],[3],[8],[3],[6],[3],[11],[9],[0],[11],[9],[7],[5],[6],[0],[9],[9],[9],[8],[9],[3],[3],[11]]]
ZW = 143
def setup_inputs(rng):
    return {"z": rng.standard_normal((N, 128, ZW), dtype=np.float32)}
def reference(z):
    y = np.zeros((N, 128, T), np.float64)
    fill = [0] * N
    for r in range(N):
        for t in range(T):
            for e in ROUTE[r][t]:
                y[r][:, t] += z[e][:, fill[e]].astype(np.float64)
                fill[e] += 1
    return {"y": y.astype(z.dtype)}

@@ -1,0 +1,275 @@
+import comms_topo
+from concourse.bass import DstId, RemoteDMATransfer
+
+WIN = 44
+BMAX = 12
+HEAD = 32
+MAXW = 2
+FINE = True
+M_CORES = (3, 2, 6, 7)
+S_CORES = (0, 1, 4, 5)
+F_OP = (0,)
+F_SP = ()
+F_HELP = (2, 6, 7, 0, 1, 4, 5)
+DEAL_PAT = ((2, 2, 2, 2, 2, 2, 2, 2),)
+DEAL_ORDER = (2, 6, 7, 0, 1, 4, 5)
+
+SCRATCH = {
+    "zs": ("sbuf", [128, 143], "float32"),
+    "pz": ("sbuf", [128, WIN], "float32"),
+    "fz": ("sbuf", [128, WIN], "float32"),
+    "asm": ("sbuf", [128, 128], "float32"),
+}
+SEMAPHORES = ["loaded", "got", "got2", "arrived", "sent", "stored"]
+
+PLAN = {}
+MEMO = {}
+
+
+def one(n, width):
+    base = 1
+    while 2 * base * n <= width:
+        base *= 2
+    up = (width - n * base) // base
+    return [2 * base] * up + [base] * (n - up)
+
+
+def split(n, width):
+    out = []
+    while n >= width:
+        out.append([1] * width)
+        n -= width
+    while n > 0:
+        pat = one(n, width)
+        slots = width // min(pat)
+        if not FINE or n >= slots - 1:
+            out.append(pat)
+            n = 0
+        else:
+            out.append([2 * min(pat)] * (slots // 2))
+            n -= slots // 2
+    return out
+
+
+def lanes(off, own, fgn, hold):
+    off = list(off)
+    on = [(u, "p") for u in own]
+    late = [(u, "f") for u in fgn]
+    calls = []
+    first = True
+    for pat in split(len(off), 8):
+        call = []
+        eng = 0
+        for n in pat:
+            call.append((off.pop(0), "p", eng, n))
+            eng += n
+        if not (first and hold):
+            on += late
+            late = []
+        first = False
+        m = min(len(on), 8 // min(pat))
+        eng = 8
+        if m:
+            for n in one(m, 8):
+                u, tag = on.pop(0)
+                call.append((u, tag, eng, n))
+                eng += n
+        calls.append(call)
+    if first and hold and on:
+        for pat in split(len(on), 16):
+            call = []
+            eng = 0
+            for n in pat:
+                u, tag = on.pop(0)
+                call.append((u, tag, eng, n))
+                eng += n
+            calls.append(call)
+    on += late
+    for pat in split(len(on), 16):
+        call = []
+        eng = 0
+        for n in pat:
+            u, tag = on.pop(0)
+            call.append((u, tag, eng, n))
+            eng += n
+        calls.append(call)
+    return calls
+
+
+def program(off, own, fgn):
+    calls = []
+    for w in range(1, MAXW + 1):
+        part = lanes([u for u in off if u[1] == w], [u for u in own if u[1] == w],
+                     [u for u in fgn if u[1] == w], w == 1)
+        calls += [(w, c) for c in part]
+    return calls
+
+
+def cost(cnt, pre):
+    key = (tuple(cnt), tuple(pre))
+    if key not in MEMO:
+        load = [0] * 16
+        for w in range(MAXW):
+            for call in lanes(range(cnt[w]), range(cnt[MAXW + w]), range(pre[w]), w == 0):
+                for tr in call:
+                    for k in range(tr[2], tr[2] + tr[3]):
+                        load[k] += 128 // tr[3]
+        MEMO[key] = max(load)
+    return MEMO[key]
+
+
+def chunks(lst, e, cores, pre, cap):
+    out = []
+    i = 0
+    for c in cores:
+        lim = cap + HEAD if c == 3 else cap
+        cnt = [0] * (2 * MAXW)
+        if cost(cnt, pre[c]) > lim:
+            return None
+        j = i
+        while j < len(lst):
+            u = lst[j]
+            cnt[(u[1] - 1) + (MAXW if u[2] == e else 0)] += 1
+            if cost(cnt, pre[c]) > lim or (c != 3 and u[0] + u[1] - lst[i][0] > WIN):
+                break
+            j += 1
+        out.append(lst[i:j])
+        i = j
+    return out if i == len(lst) else None
+
+
+def make_plan(route, zw):
+    nr = len(route)
+    nt = len(route[0])
+    units = []
+    for e in range(nr):
+        cols = [(r, t) for r in range(nr) for t in range(nt) if route[r][t][0] == e]
+        us = []
+        k = 0
+        while k < len(cols):
+            r, t = cols[k]
+            w = 1
+            while w < MAXW and k + w < len(cols) and cols[k + w] == (r, t + w):
+                w += 1
+            us.append((k, w, r, t))
+            k += w
+        units.append(us)
+    fdst = []
+    fin = [{} for r in range(nr)]
+    for e in range(nr):
+        dsts = [((e ^ 1) + 2 * j) % nr for j in F_OP] + [(e + 2 * j) % nr for j in F_SP]
+        row = []
+        for i, r in enumerate(dsts):
+            us = [u for u in units[e] if u[2] == r][:BMAX]
+            row.append((r, F_HELP[i], us))
+            fin[r][F_HELP[i]] = (e, us)
+        fdst.append(row)
+    prog = {}
+    arrived = [0] * nr
+    for e in range(nr):
+        gone = set()
+        for r, h, us in fdst[e]:
+            gone |= set(us)
+        rest = [u for u in units[e] if u not in gone]
+        xs = [u for u in rest if (u[2] ^ e) & 1]
+        ys = [u for u in rest if not (u[2] ^ e) & 1 and u[2] != e]
+        ss = [u for u in rest if u[2] == e]
+        pre = {}
+        for c in range(8):
+            us = fin[e][c][1] if c in fin[e] else []
+            pre[c] = [sum(1 for u in us if u[1] == w + 1) for w in range(MAXW)]
+        found = None
+        for cap in range(16, 4096, 16):
+            for d in range(0, min(len(ys), 24)):
+                mv = set(int((i + 0.5) * len(ys) / d) for i in range(d))
+                ml = sorted(xs + [u for i, u in enumerate(ys) if i in mv])
+                sl = sorted(ss + [u for i, u in enumerate(ys) if i not in mv])
+                m = chunks(ml, e, M_CORES, pre, cap)
+                if m is None:
+                    continue
+                s = chunks(sl, e, S_CORES, pre, cap)
+                if s is None:
+                    continue
+                found = dict(zip(M_CORES + S_CORES, m + s))
+                break
+            if found:
+                break
+        start = {}
+        for c in range(8):
+            share = found[c]
+            start[c] = 0 if c == 3 or not share else min(share[0][0], zw - WIN)
+            fsend, fus = fin[e][c] if c in fin[e] else (None, [])
+            fstart = min(fus[0][0], zw - WIN) if fus else 0
+            calls = []
+            sent = 0
+            for w, call in program([u for u in share if u[2] != e], [u for u in share if u[2] == e], fus):
+                trs = []
+                needf = False
+                for u, tag, eng, n in call:
+                    needf = needf or tag == "f"
+                    col = u[0] - (fstart if tag == "f" else start[c])
+                    trs.append((tag, col, u[2], u[3], ((1 << n) - 1) << eng))
+                    arrived[u[2]] += n
+                    sent += n
+                calls.append((w, trs, needf))
+            prog[8 * e + c] = {"calls": calls, "sent": sent, "got": 0, "got2": 0, "deal": []}
+        todo = [(8 * r + h, "fz", "got2", min(us[0][0], zw - WIN) if us else 0) for r, h, us in fdst[e]]
+        todo += [(8 * e + c, "pz", "got", start[c]) for c in DEAL_ORDER]
+        prog[8 * e + 3]["todo"] = todo
+    for e in range(nr):
+        me = prog[8 * e + 3]
+        todo = me["todo"]
+        for pat in DEAL_PAT:
+            call = []
+            eng = 0
+            for n in pat:
+                dst, buf, sem, a = todo.pop(0)
+                call.append((dst, buf, sem, a, ((1 << n) - 1) << eng))
+                prog[dst][sem] += n
+                me["sent"] += n
+                eng += n
+            me["deal"].append(call)
+    return {"prog": prog, "arrived": arrived}
+
+
+def rank_program(g, core, T, topo):
+    if "p" not in PLAN:
+        PLAN["p"] = make_plan(T.tables["ROUTE"], T.tables["ZW"])
+    me = PLAN["p"]["prog"][core]
+    sem = T.sem
+    rank = T.rank_of(core)
+
+    def to(c):
+        rid, pid, ring = topo.addr(c)
+        return [DstId(rid=rid, pnc=pid)]
+
+    if rank is not None:
+        g.sync.dma_start(T.zs[:, :], T.z[:, :]).then_inc(sem.loaded, 16)
+        g.wait_ge(sem.loaded, 16)
+        for call in me["deal"]:
+            g.remote_dma_fused(
+                [RemoteDMATransfer(dst_ids=to(dst), dma_engine_mask=mask, remote_sem=sem[s],
+                                   src=T.zs[:, a:a + WIN], dst=T[buf][:, :])
+                 for dst, buf, s, a, mask in call], local_sem=sem.sent)
+        own = T.zs
+    else:
+        g.wait_ge(sem.got, me["got"])
+        own = T.pz
+    waited = me["got2"] == 0
+    for w, trs, needf in me["calls"]:
+        if needf and not waited:
+            g.wait_ge(sem.got2, me["got2"])
+            waited = True
+        g.remote_dma_fused(
+            [RemoteDMATransfer(dst_ids=to(T.cores[r]), dma_engine_mask=mask, remote_sem=sem.arrived,
+                               src=(T.fz if tag == "f" else own)[:, col:col + w], dst=T.asm[:, t:t + w])
+             for tag, col, r, t, mask in trs], local_sem=sem.sent)
+    if not waited:
+        g.wait_ge(sem.got2, me["got2"])
+    if rank is not None:
+        g.sync.wait_ge(sem.arrived, PLAN["p"]["arrived"][rank])
+        g.sync.dma_start(T.y[:, :], T.asm[:, :]).then_inc(sem.stored, 16)
+    g.wait_ge(sem.sent, me["sent"])
+    if rank is not None:
+        g.wait_ge(sem.arrived, PLAN["p"]["arrived"][rank])
+        g.wait_ge(sem.stored, 16)

@@ -3,7 +3,8 @@ from concourse.bass import DstId, RemoteDMATransfer
 
 WIN = 44
 BMAX = 12
-HEAD = 32
+HEAD = 0
+KT = 11
 MAXW = 2
 FINE = True
 M_CORES = (3, 2, 6, 7)
@@ -130,7 +131,8 @@ def chunks(lst, e, cores, pre, cap):
         while j < len(lst):
             u = lst[j]
             cnt[(u[1] - 1) + (MAXW if u[2] == e else 0)] += 1
-            if cost(cnt, pre[c]) > lim or (c != 3 and u[0] + u[1] - lst[i][0] > WIN):
+            if cost(cnt, pre[c]) > lim or (c != 3 and KT * (sum(cnt) + sum(pre[c])) > cap) \
+                    or (c != 3 and u[0] + u[1] - lst[i][0] > WIN):
                 break
             j += 1
         out.append(lst[i:j])

import comms_topo
from concourse.bass import DstId, RemoteDMATransfer

WIN = 44
BMAX = 12
HEAD = 0
KT = 11
MAXW = 2
FINE = True
M_CORES = (3, 2, 6, 7)
S_CORES = (0, 1, 4, 5)
F_OP = (0,)
F_SP = ()
F_HELP = (2, 6, 7, 0, 1, 4, 5)
DEAL_PAT = ((2, 2, 2, 2, 2, 2, 2, 2),)
DEAL_ORDER = (2, 6, 7, 0, 1, 4, 5)

SCRATCH = {
    "zs": ("sbuf", [128, 143], "float32"),
    "pz": ("sbuf", [128, WIN], "float32"),
    "fz": ("sbuf", [128, WIN], "float32"),
    "asm": ("sbuf", [128, 128], "float32"),
}
SEMAPHORES = ["loaded", "got", "got2", "arrived", "sent", "stored"]

PLAN = {}
MEMO = {}


def one(n, width):
    base = 1
    while 2 * base * n <= width:
        base *= 2
    up = (width - n * base) // base
    return [2 * base] * up + [base] * (n - up)


def split(n, width):
    out = []
    while n >= width:
        out.append([1] * width)
        n -= width
    while n > 0:
        pat = one(n, width)
        slots = width // min(pat)
        if not FINE or n >= slots - 1:
            out.append(pat)
            n = 0
        else:
            out.append([2 * min(pat)] * (slots // 2))
            n -= slots // 2
    return out


def lanes(off, own, fgn, hold):
    off = list(off)
    on = [(u, "p") for u in own]
    late = [(u, "f") for u in fgn]
    calls = []
    first = True
    for pat in split(len(off), 8):
        call = []
        eng = 0
        for n in pat:
            call.append((off.pop(0), "p", eng, n))
            eng += n
        if not (first and hold):
            on += late
            late = []
        first = False
        m = min(len(on), 8 // min(pat))
        eng = 8
        if m:
            for n in one(m, 8):
                u, tag = on.pop(0)
                call.append((u, tag, eng, n))
                eng += n
        calls.append(call)
    if first and hold and on:
        for pat in split(len(on), 16):
            call = []
            eng = 0
            for n in pat:
                u, tag = on.pop(0)
                call.append((u, tag, eng, n))
                eng += n
            calls.append(call)
    on += late
    for pat in split(len(on), 16):
        call = []
        eng = 0
        for n in pat:
            u, tag = on.pop(0)
            call.append((u, tag, eng, n))
            eng += n
        calls.append(call)
    return calls


def program(off, own, fgn):
    calls = []
    for w in range(1, MAXW + 1):
        part = lanes([u for u in off if u[1] == w], [u for u in own if u[1] == w],
                     [u for u in fgn if u[1] == w], w == 1)
        calls += [(w, c) for c in part]
    return calls


def cost(cnt, pre):
    key = (tuple(cnt), tuple(pre))
    if key not in MEMO:
        load = [0] * 16
        for w in range(MAXW):
            for call in lanes(range(cnt[w]), range(cnt[MAXW + w]), range(pre[w]), w == 0):
                for tr in call:
                    for k in range(tr[2], tr[2] + tr[3]):
                        load[k] += 128 // tr[3]
        MEMO[key] = max(load)
    return MEMO[key]


def chunks(lst, e, cores, pre, cap):
    out = []
    i = 0
    for c in cores:
        lim = cap + HEAD if c == 3 else cap
        cnt = [0] * (2 * MAXW)
        if cost(cnt, pre[c]) > lim:
            return None
        j = i
        while j < len(lst):
            u = lst[j]
            cnt[(u[1] - 1) + (MAXW if u[2] == e else 0)] += 1
            if cost(cnt, pre[c]) > lim or (c != 3 and KT * (sum(cnt) + sum(pre[c])) > cap) \
                    or (c != 3 and u[0] + u[1] - lst[i][0] > WIN):
                break
            j += 1
        out.append(lst[i:j])
        i = j
    return out if i == len(lst) else None


def make_plan(route, zw):
    nr = len(route)
    nt = len(route[0])
    units = []
    for e in range(nr):
        cols = [(r, t) for r in range(nr) for t in range(nt) if route[r][t][0] == e]
        us = []
        k = 0
        while k < len(cols):
            r, t = cols[k]
            w = 1
            while w < MAXW and k + w < len(cols) and cols[k + w] == (r, t + w):
                w += 1
            us.append((k, w, r, t))
            k += w
        units.append(us)
    fdst = []
    fin = [{} for r in range(nr)]
    for e in range(nr):
        dsts = [((e ^ 1) + 2 * j) % nr for j in F_OP] + [(e + 2 * j) % nr for j in F_SP]
        row = []
        for i, r in enumerate(dsts):
            us = [u for u in units[e] if u[2] == r][:BMAX]
            row.append((r, F_HELP[i], us))
            fin[r][F_HELP[i]] = (e, us)
        fdst.append(row)
    prog = {}
    arrived = [0] * nr
    for e in range(nr):
        gone = set()
        for r, h, us in fdst[e]:
            gone |= set(us)
        rest = [u for u in units[e] if u not in gone]
        xs = [u for u in rest if (u[2] ^ e) & 1]
        ys = [u for u in rest if not (u[2] ^ e) & 1 and u[2] != e]
        ss = [u for u in rest if u[2] == e]
        pre = {}
        for c in range(8):
            us = fin[e][c][1] if c in fin[e] else []
            pre[c] = [sum(1 for u in us if u[1] == w + 1) for w in range(MAXW)]
        found = None
        for cap in range(16, 4096, 16):
            for d in range(0, min(len(ys), 24)):
                mv = set(int((i + 0.5) * len(ys) / d) for i in range(d))
                ml = sorted(xs + [u for i, u in enumerate(ys) if i in mv])
                sl = sorted(ss + [u for i, u in enumerate(ys) if i not in mv])
                m = chunks(ml, e, M_CORES, pre, cap)
                if m is None:
                    continue
                s = chunks(sl, e, S_CORES, pre, cap)
                if s is None:
                    continue
                found = dict(zip(M_CORES + S_CORES, m + s))
                break
            if found:
                break
        start = {}
        for c in range(8):
            share = found[c]
            start[c] = 0 if c == 3 or not share else min(share[0][0], zw - WIN)
            fsend, fus = fin[e][c] if c in fin[e] else (None, [])
            fstart = min(fus[0][0], zw - WIN) if fus else 0
            calls = []
            sent = 0
            for w, call in program([u for u in share if u[2] != e], [u for u in share if u[2] == e], fus):
                trs = []
                needf = False
                for u, tag, eng, n in call:
                    needf = needf or tag == "f"
                    col = u[0] - (fstart if tag == "f" else start[c])
                    trs.append((tag, col, u[2], u[3], ((1 << n) - 1) << eng))
                    arrived[u[2]] += n
                    sent += n
                calls.append((w, trs, needf))
            prog[8 * e + c] = {"calls": calls, "sent": sent, "got": 0, "got2": 0, "deal": []}
        todo = [(8 * r + h, "fz", "got2", min(us[0][0], zw - WIN) if us else 0) for r, h, us in fdst[e]]
        todo += [(8 * e + c, "pz", "got", start[c]) for c in DEAL_ORDER]
        prog[8 * e + 3]["todo"] = todo
    for e in range(nr):
        me = prog[8 * e + 3]
        todo = me["todo"]
        for pat in DEAL_PAT:
            call = []
            eng = 0
            for n in pat:
                dst, buf, sem, a = todo.pop(0)
                call.append((dst, buf, sem, a, ((1 << n) - 1) << eng))
                prog[dst][sem] += n
                me["sent"] += n
                eng += n
            me["deal"].append(call)
    return {"prog": prog, "arrived": arrived}


def rank_program(g, core, T, topo):
    if "p" not in PLAN:
        PLAN["p"] = make_plan(T.tables["ROUTE"], T.tables["ZW"])
    me = PLAN["p"]["prog"][core]
    sem = T.sem
    rank = T.rank_of(core)

    def to(c):
        rid, pid, ring = topo.addr(c)
        return [DstId(rid=rid, pnc=pid)]

    if rank is not None:
        g.sync.dma_start(T.zs[:, :], T.z[:, :]).then_inc(sem.loaded, 16)
        g.wait_ge(sem.loaded, 16)
        for call in me["deal"]:
            g.remote_dma_fused(
                [RemoteDMATransfer(dst_ids=to(dst), dma_engine_mask=mask, remote_sem=sem[s],
                                   src=T.zs[:, a:a + WIN], dst=T[buf][:, :])
                 for dst, buf, s, a, mask in call], local_sem=sem.sent)
        own = T.zs
    else:
        g.wait_ge(sem.got, me["got"])
        own = T.pz
    waited = me["got2"] == 0
    for w, trs, needf in me["calls"]:
        if needf and not waited:
            g.wait_ge(sem.got2, me["got2"])
            waited = True
        g.remote_dma_fused(
            [RemoteDMATransfer(dst_ids=to(T.cores[r]), dma_engine_mask=mask, remote_sem=sem.arrived,
                               src=(T.fz if tag == "f" else own)[:, col:col + w], dst=T.asm[:, t:t + w])
             for tag, col, r, t, mask in trs], local_sem=sem.sent)
    if not waited:
        g.wait_ge(sem.got2, me["got2"])
    if rank is not None:
        g.sync.wait_ge(sem.arrived, PLAN["p"]["arrived"][rank])
        g.sync.dma_start(T.y[:, :], T.asm[:, :]).then_inc(sem.stored, 16)
    g.wait_ge(sem.sent, me["sent"])
    if rank is not None:
        g.wait_ge(sem.arrived, PLAN["p"]["arrived"][rank])
        g.wait_ge(sem.stored, 16)
